import numpy as np
import ml_dtypes


def mxq(x, axis, fmt="e4m3"):
    dtype, down = {"e4m3": (ml_dtypes.float8_e4m3fn, 7), "e5m2": (ml_dtypes.float8_e5m2, 14)}[fmt]
    v = np.moveaxis(np.asarray(x, np.float32).astype(ml_dtypes.bfloat16).astype(np.float64), axis, -1)
    blocks = v.reshape(v.shape[:-1] + (-1, 32))
    amax = np.abs(blocks).max(-1, keepdims=True)
    byte = np.maximum(np.where(amax > 0, np.frexp(amax)[1] - 1 + 127, 0) - down, 1)
    scale = np.exp2(byte - 127.0)
    codes = (blocks / scale).astype(np.float32).astype(dtype).astype(np.float64)
    return np.moveaxis((codes * scale).reshape(v.shape), -1, axis)


WIDE = False


def mx_kscale(k):
    if not WIDE:
        return np.ones(k)
    levels = np.array([10, -10, 5, -5, 0])
    if k % 512:
        return np.exp2(np.random.permutation(np.resize(levels, k // 32))).repeat(32)
    a = np.empty((k // 512, 16))
    for p in range(k // 512):
        a[p, :8] = np.random.permutation(np.resize(levels, 8))
        for g in range(8):
            far = levels[np.abs(levels - a[p, g]) >= 10]
            a[p, g + 8] = far[np.random.randint(len(far))]
    return np.exp2(a.ravel()).repeat(32)


def f64(x):
    return np.asarray(x).astype(np.float64)


def striped(idx):
    return np.tile(idx.reshape(-1, 16).T, (8, 1)).astype(np.uint16)


def unstriped(offs):
    return offs[:16].T.reshape(-1).astype(np.int64)


def pack_weight(w):
    k, n = w.shape
    w = f64(np.asarray(w, np.float32).astype(ml_dtypes.bfloat16)).reshape(k // 32, 32, n)
    amax = np.abs(w).max(1)
    byte = np.clip(np.where(amax > 0, np.frexp(amax)[1] - 1 + 127 - 7, 1), 1, 254)
    scaled = (w * np.exp2(127.0 - byte)[:, None, :]).reshape(k, n).astype(np.float32)
    words = np.ascontiguousarray(scaled.reshape(k // 512, 128, 4, n).transpose(0, 1, 3, 2)).astype(ml_dtypes.float8_e4m3fn).view(np.uint8)
    return words, np.ascontiguousarray(byte.astype(np.uint8).reshape(k // 512, 16, n))


def unpack_weight(words, scales):
    g, p, n, _ = words.shape
    vals = np.ascontiguousarray(words).view(ml_dtypes.float8_e4m3fn).astype(np.float64) * np.repeat(np.exp2(scales.astype(np.float64) - 127.0), 8, axis=1)[..., None]
    return vals.transpose(0, 1, 3, 2).reshape(g * 512, n)


def relu(v):
    return np.maximum(v, 0.0)


K, T, S, N, U = 512, 2048, 512, 256, 1024


def setup_inputs():
    n = np.random.standard_normal
    s = mx_kscale(K)[:, None]
    packed_xT = pack_weight(n((K, T)) * s)
    return {
        "x_words": packed_xT[0],
        "x_scales": packed_xT[1],
        "w1": (n((K, N)) / np.sqrt(K) / s).astype(np.float32),
        "w2": (n((K, N)) / np.sqrt(K) / s).astype(np.float32),
        "cmap": (n((N, U)) * 0.7).astype(np.float32),
        "thr": (-np.random.uniform(0.3, 1.0, (N, 1))).astype(np.float32),
        "offs": striped(np.random.permutation(T)[:S]),
        "cell": striped(np.random.permutation(U)[:S]),
    }


def reference(x_words, x_scales, w1, w2, cmap, thr, offs, cell):
    xq = unpack_weight(x_words, x_scales)[:, unstriped(offs)]
    z = np.log(((mxq(f64(w1), 0, "e4m3").T @ xq)) ** 2 + ((mxq(f64(w2), 0, "e4m3").T @ xq)) ** 2 + 0.1)
    m0 = f64(cmap)[:, unstriped(cell)]
    df = z - m0
    return relu(df + f64(thr))

@@ -1,0 +1,142 @@
+from contextlib import ExitStack
+
+import concourse.mybir as mybir
+
+K, T, S, N, U = 512, 2048, 512, 256, 1024
+FLOPS = 2 * 2 * K * N * S
+
+F32 = mybir.dt.float32
+BF16 = mybir.dt.bfloat16
+I32 = mybir.dt.int32
+U32 = mybir.dt.uint32
+U16 = mybir.dt.uint16
+U8 = mybir.dt.uint8
+FP8X4 = mybir.dt.float8_e4m3fn_x4
+ACT = mybir.ActivationFunctionType
+ALU = mybir.AluOpType
+
+P = 128
+PACK = 4
+HALF = S // 2
+
+
+def tile_picked_yclut_det_p_kernel(tc, x_words, x_scales, w1, w2, cmap, thr, offs, cell, out):
+    nc = tc.nc
+    with ExitStack() as ctx:
+        keep = ctx.enter_context(tc.tile_pool(name="keep", bufs=1))
+        psum = ctx.enter_context(tc.psum_pool(name="psum", bufs=1))
+        late = ctx.enter_context(tc.tile_pool(name="late", bufs=1))
+        share = ctx.enter_context(tc.tile_pool(name="share", bufs=1))
+
+        offs_t = keep.tile([P, S // 16], U16, name="offs_t")
+        cell_t = keep.tile([P, S // 16], U16, name="cell_t")
+        planes = share.tile([P, T], U8, name="planes", align_bytes=64, offset=0)
+        ident = keep.tile([P, P], F32, name="ident")
+        zeros = late.tile([P, 5 * U + 8], F32, name="zeros", offset=0)
+        raw1 = keep.tile([P, PACK, N], F32, name="raw1")
+
+        nc.vector.memset(planes[:].bitcast(I32), 0)
+        nc.vector.memset(zeros[:, :P], 0.0)
+        nc.sync.dma_start(out=raw1[:], in_=w1.rearrange("(p j) n -> p j n", j=PACK))
+        nc.sync.dma_start(offs_t[:], offs)
+        nc.sync.dma_start(cell_t[:], cell)
+        for q in range(4):
+            nc.scalar.dma_start(out=planes[32 * q : 32 * q + 4, :].bitcast(I32), in_=x_scales[0, 4 * q : 4 * q + 4, :].bitcast(I32))
+        nc.gpsimd.affine_select(out=ident[:], in_=zeros[:, :P], compare_op=ALU.not_equal, fill=1.0, base=0, pattern=[[-1, P]], channel_multiplier=1)
+        raw2 = late.tile([P, PACK, N], F32, name="raw2", offset=0)
+        cm = [late.tile([P, U], F32, name="cm%d" % b, offset=(1 + b) * 4 * U) for b in range(2)]
+        thr_t = late.tile([P, 2], F32, name="thr_t", offset=20 * U)
+        words = late.tile([P, T], U32, name="words", offset=12 * U)
+        nc.sync.dma_start(out=words[:].bitcast(I32), in_=x_words[0].rearrange("p n t -> p (n t)").bitcast(I32))
+        nc.sync.dma_start(out=raw2[:], in_=w2.rearrange("(p j) n -> p j n", j=PACK))
+        for b in range(2):
+            nc.sync.dma_start(out=cm[b][:], in_=cmap[b * P : (b + 1) * P, :])
+        with nc.allow_non_contiguous_dma(reason="one threshold a row"):
+            nc.sync.dma_start(out=thr_t[:], in_=thr.rearrange("(b p) o -> p (b o)", p=P))
+
+        def interleave(copy, dst, src):
+            copy(out=dst.rearrange("p (c e) t -> p c t e", e=4), in_=src.rearrange("p t (c e) -> p c t e", e=4))
+
+        grouped1 = keep.tile([P, N, PACK], BF16, name="grouped1", align_bytes=64)
+        codes1 = keep.tile([P, N], U32, name="codes1", align_bytes=64)
+        scales1 = keep.tile([P, N], U8, name="scales1", align_bytes=64)
+        interleave(nc.vector.tensor_copy, grouped1[:, :128, :], raw1[:, :, :128])
+        interleave(nc.scalar.copy, grouped1[:, 128:, :], raw1[:, :, 128:])
+        nc.vector.quantize_mx(out=codes1[:].bitcast(FP8X4), scales=scales1[:], in_=grouped1[:].rearrange("p n t -> p (n t)"))
+
+        xs = keep.tile([P, S], U8, name="xs", align_bytes=64)
+        nc.vector.tensor_copy(xs[:], planes[:].indirect(offs_t[:]))
+        xw = []
+        for h in range(2):
+            picked = share.tile([P, HALF], U32, name="xw%d" % h, align_bytes=64, offset=4 * HALF * h)
+            nc.vector.tensor_copy(picked[:], words[:].indirect(offs_t[:, h * HALF // 16 : (h + 1) * HALF // 16]))
+            xw.append(picked)
+
+        def product(dst, jt, codes, scales):
+            h, r = divmod(jt, 2)
+            nc.tensor.matmul_mx(
+                out=dst, lhsT=xw[h][:, r * P : (r + 1) * P].bitcast(FP8X4), lhsT_scale=xs[:, jt * P : (jt + 1) * P],
+                rhs=codes[:].bitcast(FP8X4), rhs_scale=scales[:], start=True, stop=True,
+            )
+
+        power = [[], []]
+
+        def turn(b, jt, src, start, stop):
+            h, r = divmod(jt, 2)
+            nc.tensor.matmul(power[b][h][:, r, :], lhsT=src, rhs=ident[:], is_transpose=True, start=start, stop=stop)
+
+        sq1 = []
+        for h in range(2):
+            prod = psum.tile([P, 2, N], F32, name="prod1%d" % h)
+            for r in range(2):
+                product(prod[:, r, :], 2 * h + r, codes1, scales1)
+            sq = keep.tile([P, 2, N], F32, name="sq1%d" % h)
+            nc.scalar.activation(out=sq[:], in_=prod[:], func=ACT.Square)
+            sq1.append(sq)
+
+        grouped2 = [share.tile([P, P, PACK], BF16, name="grouped2%d" % b, align_bytes=64, offset=2048 + 1536 * b) for b in range(2)]
+        for b in range(2):
+            interleave(nc.vector.tensor_copy, grouped2[b][:], raw2[:, :, b * P : (b + 1) * P])
+        sq2 = []
+        for b in range(2):
+            codes = keep.tile([P, P], U32, name="codes2%d" % b, align_bytes=64)
+            scales = keep.tile([P, P], U8, name="scales2%d" % b, align_bytes=64)
+            nc.vector.quantize_mx(out=codes[:].bitcast(FP8X4), scales=scales[:], in_=grouped2[b][:].rearrange("p n t -> p (n t)"))
+            sq = keep.tile([P, 4, P], F32, name="sq2%d" % b)
+            for h in range(2):
+                prod = psum.tile([P, 2, P], F32, name="prod2", tag="bank%d%d" % (b, h))
+                for r in range(2):
+                    product(prod[:, r, :], 2 * h + r, codes, scales)
+                nc.scalar.activation(out=sq[:, 2 * h : 2 * h + 2, :], in_=prod[:], func=ACT.Square)
+            sq2.append(sq)
+        for b in range(2):
+            for h in range(2):
+                power[b].append(psum.tile([P, 2, P], F32, name="power", tag="bank%d%d" % (b, h)))
+
+        for b in range(2):
+            for h in range(2):
+                for r in range(2):
+                    turn(b, 2 * h + r, sq1[h][:, r, b * P : (b + 1) * P], r == 0, False)
+                for r in range(2):
+                    turn(b, 2 * h + r, sq2[b][:, 2 * h + r, :], False, r == 1)
+
+        clutter = []
+        for b in range(2):
+            g = share.tile([P, S], F32, name="g%d" % b, offset=2048 + 2048 * b)
+            nc.vector.tensor_copy(g[:], cm[b][:].indirect(cell_t[:]))
+            clutter.append(g)
+        pieces = [(b, h) for b in range(2) for h in range(2)]
+        z = {}
+        for b, h in pieces:
+            z[b, h] = keep.tile([P, HALF], F32, name="z%d%d" % (b, h))
+            nc.scalar.activation(out=z[b, h][:], in_=power[b][h][:].rearrange("p r n -> p (r n)"), func=ACT.Ln, bias=0.1)
+        for b, h in pieces:
+            cols = slice(h * HALF, (h + 1) * HALF)
+            df = keep.tile([P, HALF], F32, name="df%d%d" % (b, h))
+            nc.vector.scalar_tensor_tensor(out=df[:], in0=z[b, h][:], scalar=thr_t[:, b : b + 1], in1=clutter[b][:, cols], op0=ALU.add, op1=ALU.subtract)
+            res = keep.tile([P, HALF], F32, name="res%d%d" % (b, h))
+            if False:
+                nc.scalar.activation(out=res[:], in_=df[:], func=ACT.Relu)
+            else:
+                nc.vector.tensor_scalar(out=res[:], in0=df[:], scalar1=0.0, scalar2=None, op0=ALU.max)
+            nc.sync.dma_start(out=out[b * P : (b + 1) * P, cols], in_=res[:])

@@ -37,12 +37,16 @@ def tile_picked_yclut_det_p_kernel(tc, x_words, x_scales, w1, w2, cmap, thr, off
 
         nc.vector.memset(planes[:].bitcast(I32), 0)
         nc.vector.memset(zeros[:, :P], 0.0)
+        warm_in = keep.tile([P, 1], F32, name="warm_in")
+        nc.vector.memset(warm_in[:], 1.0)
         nc.sync.dma_start(out=raw1[:], in_=w1.rearrange("(p j) n -> p j n", j=PACK))
         nc.sync.dma_start(offs_t[:], offs)
         nc.sync.dma_start(cell_t[:], cell)
         for q in range(4):
             nc.scalar.dma_start(out=planes[32 * q : 32 * q + 4, :].bitcast(I32), in_=x_scales[0, 4 * q : 4 * q + 4, :].bitcast(I32))
         nc.gpsimd.affine_select(out=ident[:], in_=zeros[:, :P], compare_op=ALU.not_equal, fill=1.0, base=0, pattern=[[-1, P]], channel_multiplier=1)
+        warm_out = keep.tile([P, 1], F32, name="warm_out")
+        nc.scalar.activation(out=warm_out[:], in_=warm_in[:], func=ACT.Ln)
         raw2 = late.tile([P, PACK, N], F32, name="raw2", offset=0)
         cm = [late.tile([P, U], F32, name="cm%d" % b, offset=(1 + b) * 4 * U) for b in range(2)]
         thr_t = late.tile([P, 2], F32, name="thr_t", offset=20 * U)

@@ -32,8 +32,9 @@ def tile_picked_yclut_det_p_kernel(tc, x_words, x_scales, w1, w2, cmap, thr, off
         cell_t = keep.tile([P, S // 16], U16, name="cell_t")
         planes = share.tile([P, T], U8, name="planes", align_bytes=64, offset=0)
         ident = keep.tile([P, P], F32, name="ident")
-        zeros = late.tile([P, 5 * U + 8], F32, name="zeros", offset=0)
+        zeros = late.tile([P, 3 * U + 8], F32, name="zeros", offset=0)
         raw1 = keep.tile([P, PACK, N], F32, name="raw1")
+        words = keep.tile([P, T], U32, name="words", align_bytes=64)
 
         nc.vector.memset(planes[:].bitcast(I32), 0)
         nc.vector.memset(zeros[:, :P], 0.0)
@@ -41,6 +42,7 @@ def tile_picked_yclut_det_p_kernel(tc, x_words, x_scales, w1, w2, cmap, thr, off
         nc.vector.memset(warm_in[:], 1.0)
         nc.sync.dma_start(out=raw1[:], in_=w1.rearrange("(p j) n -> p j n", j=PACK))
         nc.sync.dma_start(offs_t[:], offs)
+        nc.sync.dma_start(out=words[:].bitcast(I32), in_=x_words[0].rearrange("p n t -> p (n t)").bitcast(I32))
         nc.sync.dma_start(cell_t[:], cell)
         for q in range(4):
             nc.scalar.dma_start(out=planes[32 * q : 32 * q + 4, :].bitcast(I32), in_=x_scales[0, 4 * q : 4 * q + 4, :].bitcast(I32))
@@ -49,9 +51,7 @@ def tile_picked_yclut_det_p_kernel(tc, x_words, x_scales, w1, w2, cmap, thr, off
         nc.scalar.activation(out=warm_out[:], in_=warm_in[:], func=ACT.Ln)
         raw2 = late.tile([P, PACK, N], F32, name="raw2", offset=0)
         cm = [late.tile([P, U], F32, name="cm%d" % b, offset=(1 + b) * 4 * U) for b in range(2)]
-        thr_t = late.tile([P, 2], F32, name="thr_t", offset=20 * U)
-        words = late.tile([P, T], U32, name="words", offset=12 * U)
-        nc.sync.dma_start(out=words[:].bitcast(I32), in_=x_words[0].rearrange("p n t -> p (n t)").bitcast(I32))
+        thr_t = late.tile([P, 2], F32, name="thr_t", offset=12 * U)
         nc.sync.dma_start(out=raw2[:], in_=w2.rearrange("(p j) n -> p j n", j=PACK))
         for b in range(2):
             nc.sync.dma_start(out=cm[b][:], in_=cmap[b * P : (b + 1) * P, :])
@@ -83,64 +83,73 @@ def tile_picked_yclut_det_p_kernel(tc, x_words, x_scales, w1, w2, cmap, thr, off
                 rhs=codes[:].bitcast(FP8X4), rhs_scale=scales[:], start=True, stop=True,
             )
 
-        power = [[], []]
-
-        def turn(b, jt, src, start, stop):
-            h, r = divmod(jt, 2)
-            nc.tensor.matmul(power[b][h][:, r, :], lhsT=src, rhs=ident[:], is_transpose=True, start=start, stop=stop)
-
+        grouped2 = share.tile([P, N, PACK], BF16, name="grouped2", align_bytes=64, offset=3072)
+        interleave(nc.vector.tensor_copy, grouped2[:, :160, :], raw2[:, :, :160])
+        interleave(nc.scalar.copy, grouped2[:, 160:, :], raw2[:, :, 160:])
         sq1 = []
         for h in range(2):
             prod = psum.tile([P, 2, N], F32, name="prod1%d" % h)
             for r in range(2):
                 product(prod[:, r, :], 2 * h + r, codes1, scales1)
-            sq = keep.tile([P, 2, N], F32, name="sq1%d" % h)
+            sq = late.tile([P, 2, N], F32, name="sq1%d" % h, offset=8 * N * h)
             nc.scalar.activation(out=sq[:], in_=prod[:], func=ACT.Square)
             sq1.append(sq)
 
-        grouped2 = [share.tile([P, P, PACK], BF16, name="grouped2%d" % b, align_bytes=64, offset=2048 + 1536 * b) for b in range(2)]
-        for b in range(2):
-            interleave(nc.vector.tensor_copy, grouped2[b][:], raw2[:, :, b * P : (b + 1) * P])
-        sq2 = []
+        pieces = [(b, h) for b in range(2) for h in range(2)]
+        quantised2 = []
         for b in range(2):
             codes = keep.tile([P, P], U32, name="codes2%d" % b, align_bytes=64)
             scales = keep.tile([P, P], U8, name="scales2%d" % b, align_bytes=64)
-            nc.vector.quantize_mx(out=codes[:].bitcast(FP8X4), scales=scales[:], in_=grouped2[b][:].rearrange("p n t -> p (n t)"))
-            sq = keep.tile([P, 4, P], F32, name="sq2%d" % b)
-            for h in range(2):
-                prod = psum.tile([P, 2, P], F32, name="prod2", tag="bank%d%d" % (b, h))
-                for r in range(2):
-                    product(prod[:, r, :], 2 * h + r, codes, scales)
-                nc.scalar.activation(out=sq[:, 2 * h : 2 * h + 2, :], in_=prod[:], func=ACT.Square)
-            sq2.append(sq)
-        for b in range(2):
-            for h in range(2):
-                power[b].append(psum.tile([P, 2, P], F32, name="power", tag="bank%d%d" % (b, h)))
-
-        for b in range(2):
-            for h in range(2):
-                for r in range(2):
-                    turn(b, 2 * h + r, sq1[h][:, r, b * P : (b + 1) * P], r == 0, False)
-                for r in range(2):
-                    turn(b, 2 * h + r, sq2[b][:, 2 * h + r, :], False, r == 1)
+            nc.vector.quantize_mx(out=codes[:].bitcast(FP8X4), scales=scales[:], in_=grouped2[:, b * P : (b + 1) * P, :].rearrange("p n t -> p (n t)"))
+            quantised2.append((codes, scales))
 
         clutter = []
         for b in range(2):
             g = share.tile([P, S], F32, name="g%d" % b, offset=2048 + 2048 * b)
             nc.vector.tensor_copy(g[:], cm[b][:].indirect(cell_t[:]))
             clutter.append(g)
-        pieces = [(b, h) for b in range(2) for h in range(2)]
-        z = {}
-        for b, h in pieces:
+
+        sq2, z, df = {}, {}, {}
+
+        def square(b, h):
+            prod = psum.tile([P, 2, P], F32, name="prod2", tag="bank%d%d" % (b, h))
+            for r in range(2):
+                product(prod[:, r, :], 2 * h + r, *quantised2[b])
+            sq2[b, h] = keep.tile([P, 2, P], F32, name="sq2", tag="piece%d%d" % (b, h))
+            nc.scalar.activation(out=sq2[b, h][:], in_=prod[:], func=ACT.Square)
+
+        def log_power(b, h):
+            power = psum.tile([P, 2, P], F32, name="power", tag="bank%d%d" % (b, h))
+            for r in range(2):
+                nc.tensor.matmul(power[:, r, :], lhsT=sq1[h][:, r, b * P : (b + 1) * P], rhs=ident[:], is_transpose=True, start=r == 0, stop=False)
+            for r in range(2):
+                nc.tensor.matmul(power[:, r, :], lhsT=sq2[b, h][:, r, :], rhs=ident[:], is_transpose=True, start=False, stop=r == 1)
             z[b, h] = keep.tile([P, HALF], F32, name="z%d%d" % (b, h))
-            nc.scalar.activation(out=z[b, h][:], in_=power[b][h][:].rearrange("p r n -> p (r n)"), func=ACT.Ln, bias=0.1)
-        for b, h in pieces:
-            cols = slice(h * HALF, (h + 1) * HALF)
-            df = keep.tile([P, HALF], F32, name="df%d%d" % (b, h))
-            nc.vector.scalar_tensor_tensor(out=df[:], in0=z[b, h][:], scalar=thr_t[:, b : b + 1], in1=clutter[b][:, cols], op0=ALU.add, op1=ALU.subtract)
-            res = keep.tile([P, HALF], F32, name="res%d%d" % (b, h))
-            if False:
-                nc.scalar.activation(out=res[:], in_=df[:], func=ACT.Relu)
+            nc.scalar.activation(out=z[b, h][:], in_=power[:].rearrange("p r n -> p (r n)"), func=ACT.Ln, bias=0.1)
+
+        def excess(b, h):
+            df[b, h] = keep.tile([P, HALF], F32, name="df%d%d" % (b, h))
+            nc.vector.scalar_tensor_tensor(
+                out=df[b, h][:], in0=z[b, h][:], scalar=thr_t[:, b : b + 1], in1=clutter[b][:, h * HALF : (h + 1) * HALF],
+                op0=ALU.add, op1=ALU.subtract,
+            )
+
+        def finish(b, h):
+            if b == h:
+                res = keep.tile([P, HALF], F32, name="res%d%d" % (b, h))
+                nc.vector.tensor_scalar(out=res[:], in0=df[b, h][:], scalar1=0.0, scalar2=None, op0=ALU.max)
             else:
-                nc.vector.tensor_scalar(out=res[:], in0=df[:], scalar1=0.0, scalar2=None, op0=ALU.max)
-            nc.sync.dma_start(out=out[b * P : (b + 1) * P, cols], in_=res[:])
+                res = keep.tile([P, HALF], F32, name="res", tag="piece%d1" % (1 - b))
+                nc.scalar.activation(out=res[:], in_=df[b, h][:], func=ACT.Relu)
+            nc.sync.dma_start(out=out[b * P : (b + 1) * P, h * HALF : (h + 1) * HALF], in_=res[:])
+
+        for i in range(len(pieces) + 3):
+            if i >= 3:
+                log_power(*pieces[i - 3])
+            if i < len(pieces):
+                square(*pieces[i])
+        for i in range(len(pieces) + 1):
+            if i < len(pieces):
+                excess(*pieces[i])
+            if i >= 1:
+                finish(*pieces[i - 1])

@@ -32,9 +32,8 @@ def tile_picked_yclut_det_p_kernel(tc, x_words, x_scales, w1, w2, cmap, thr, off
         cell_t = keep.tile([P, S // 16], U16, name="cell_t")
         planes = share.tile([P, T], U8, name="planes", align_bytes=64, offset=0)
         ident = keep.tile([P, P], F32, name="ident")
-        zeros = late.tile([P, 3 * U + 8], F32, name="zeros", offset=0)
+        zeros = late.tile([P, 5 * U + 8], F32, name="zeros", offset=0)
         raw1 = keep.tile([P, PACK, N], F32, name="raw1")
-        words = keep.tile([P, T], U32, name="words", align_bytes=64)
 
         nc.vector.memset(planes[:].bitcast(I32), 0)
         nc.vector.memset(zeros[:, :P], 0.0)
@@ -42,7 +41,6 @@ def tile_picked_yclut_det_p_kernel(tc, x_words, x_scales, w1, w2, cmap, thr, off
         nc.vector.memset(warm_in[:], 1.0)
         nc.sync.dma_start(out=raw1[:], in_=w1.rearrange("(p j) n -> p j n", j=PACK))
         nc.sync.dma_start(offs_t[:], offs)
-        nc.sync.dma_start(out=words[:].bitcast(I32), in_=x_words[0].rearrange("p n t -> p (n t)").bitcast(I32))
         nc.sync.dma_start(cell_t[:], cell)
         for q in range(4):
             nc.scalar.dma_start(out=planes[32 * q : 32 * q + 4, :].bitcast(I32), in_=x_scales[0, 4 * q : 4 * q + 4, :].bitcast(I32))
@@ -51,7 +49,9 @@ def tile_picked_yclut_det_p_kernel(tc, x_words, x_scales, w1, w2, cmap, thr, off
         nc.scalar.activation(out=warm_out[:], in_=warm_in[:], func=ACT.Ln)
         raw2 = late.tile([P, PACK, N], F32, name="raw2", offset=0)
         cm = [late.tile([P, U], F32, name="cm%d" % b, offset=(1 + b) * 4 * U) for b in range(2)]
-        thr_t = late.tile([P, 2], F32, name="thr_t", offset=12 * U)
+        thr_t = late.tile([P, 2], F32, name="thr_t", offset=20 * U)
+        words = late.tile([P, T], U32, name="words", offset=12 * U)
+        nc.sync.dma_start(out=words[:].bitcast(I32), in_=x_words[0].rearrange("p n t -> p (n t)").bitcast(I32))
         nc.sync.dma_start(out=raw2[:], in_=w2.rearrange("(p j) n -> p j n", j=PACK))
         for b in range(2):
             nc.sync.dma_start(out=cm[b][:], in_=cmap[b * P : (b + 1) * P, :])

from contextlib import ExitStack

import concourse.mybir as mybir

K, T, S, N, U = 512, 2048, 512, 256, 1024
FLOPS = 2 * 2 * K * N * S

F32 = mybir.dt.float32
BF16 = mybir.dt.bfloat16
I32 = mybir.dt.int32
U32 = mybir.dt.uint32
U16 = mybir.dt.uint16
U8 = mybir.dt.uint8
FP8X4 = mybir.dt.float8_e4m3fn_x4
ACT = mybir.ActivationFunctionType
ALU = mybir.AluOpType

P = 128
PACK = 4
HALF = S // 2


def tile_picked_yclut_det_p_kernel(tc, x_words, x_scales, w1, w2, cmap, thr, offs, cell, out):
    nc = tc.nc
    with ExitStack() as ctx:
        keep = ctx.enter_context(tc.tile_pool(name="keep", bufs=1))
        psum = ctx.enter_context(tc.psum_pool(name="psum", bufs=1))
        late = ctx.enter_context(tc.tile_pool(name="late", bufs=1))
        share = ctx.enter_context(tc.tile_pool(name="share", bufs=1))

        offs_t = keep.tile([P, S // 16], U16, name="offs_t")
        cell_t = keep.tile([P, S // 16], U16, name="cell_t")
        planes = share.tile([P, T], U8, name="planes", align_bytes=64, offset=0)
        ident = keep.tile([P, P], F32, name="ident")
        zeros = late.tile([P, 5 * U + 8], F32, name="zeros", offset=0)
        raw1 = keep.tile([P, PACK, N], F32, name="raw1")

        nc.vector.memset(planes[:].bitcast(I32), 0)
        nc.vector.memset(zeros[:, :P], 0.0)
        warm_in = keep.tile([P, 1], F32, name="warm_in")
        nc.vector.memset(warm_in[:], 1.0)
        nc.sync.dma_start(out=raw1[:], in_=w1.rearrange("(p j) n -> p j n", j=PACK))
        nc.sync.dma_start(offs_t[:], offs)
        nc.sync.dma_start(cell_t[:], cell)
        for q in range(4):
            nc.scalar.dma_start(out=planes[32 * q : 32 * q + 4, :].bitcast(I32), in_=x_scales[0, 4 * q : 4 * q + 4, :].bitcast(I32))
        nc.gpsimd.affine_select(out=ident[:], in_=zeros[:, :P], compare_op=ALU.not_equal, fill=1.0, base=0, pattern=[[-1, P]], channel_multiplier=1)
        warm_out = keep.tile([P, 1], F32, name="warm_out")
        nc.scalar.activation(out=warm_out[:], in_=warm_in[:], func=ACT.Ln)
        raw2 = late.tile([P, PACK, N], F32, name="raw2", offset=0)
        cm = [late.tile([P, U], F32, name="cm%d" % b, offset=(1 + b) * 4 * U) for b in range(2)]
        thr_t = late.tile([P, 2], F32, name="thr_t", offset=20 * U)
        words = late.tile([P, T], U32, name="words", offset=12 * U)
        nc.sync.dma_start(out=words[:].bitcast(I32), in_=x_words[0].rearrange("p n t -> p (n t)").bitcast(I32))
        nc.sync.dma_start(out=raw2[:], in_=w2.rearrange("(p j) n -> p j n", j=PACK))
        for b in range(2):
            nc.sync.dma_start(out=cm[b][:], in_=cmap[b * P : (b + 1) * P, :])
        with nc.allow_non_contiguous_dma(reason="one threshold a row"):
            nc.sync.dma_start(out=thr_t[:], in_=thr.rearrange("(b p) o -> p (b o)", p=P))

        def interleave(copy, dst, src):
            copy(out=dst.rearrange("p (c e) t -> p c t e", e=4), in_=src.rearrange("p t (c e) -> p c t e", e=4))

        grouped1 = keep.tile([P, N, PACK], BF16, name="grouped1", align_bytes=64)
        codes1 = keep.tile([P, N], U32, name="codes1", align_bytes=64)
        scales1 = keep.tile([P, N], U8, name="scales1", align_bytes=64)
        interleave(nc.vector.tensor_copy, grouped1[:, :128, :], raw1[:, :, :128])
        interleave(nc.scalar.copy, grouped1[:, 128:, :], raw1[:, :, 128:])
        nc.vector.quantize_mx(out=codes1[:].bitcast(FP8X4), scales=scales1[:], in_=grouped1[:].rearrange("p n t -> p (n t)"))

        xs = keep.tile([P, S], U8, name="xs", align_bytes=64)
        nc.vector.tensor_copy(xs[:], planes[:].indirect(offs_t[:]))
        xw = []
        for h in range(2):
            picked = share.tile([P, HALF], U32, name="xw%d" % h, align_bytes=64, offset=4 * HALF * h)
            nc.vector.tensor_copy(picked[:], words[:].indirect(offs_t[:, h * HALF // 16 : (h + 1) * HALF // 16]))
            xw.append(picked)

        def product(dst, jt, codes, scales):
            h, r = divmod(jt, 2)
            nc.tensor.matmul_mx(
                out=dst, lhsT=xw[h][:, r * P : (r + 1) * P].bitcast(FP8X4), lhsT_scale=xs[:, jt * P : (jt + 1) * P],
                rhs=codes[:].bitcast(FP8X4), rhs_scale=scales[:], start=True, stop=True,
            )

        grouped2 = share.tile([P, N, PACK], BF16, name="grouped2", align_bytes=64, offset=3072)
        interleave(nc.vector.tensor_copy, grouped2[:, :160, :], raw2[:, :, :160])
        interleave(nc.scalar.copy, grouped2[:, 160:, :], raw2[:, :, 160:])
        sq1 = []
        for h in range(2):
            prod = psum.tile([P, 2, N], F32, name="prod1%d" % h)
            for r in range(2):
                product(prod[:, r, :], 2 * h + r, codes1, scales1)
            sq = late.tile([P, 2, N], F32, name="sq1%d" % h, offset=8 * N * h)
            nc.scalar.activation(out=sq[:], in_=prod[:], func=ACT.Square)
            sq1.append(sq)

        pieces = [(b, h) for b in range(2) for h in range(2)]
        quantised2 = []
        for b in range(2):
            codes = keep.tile([P, P], U32, name="codes2%d" % b, align_bytes=64)
            scales = keep.tile([P, P], U8, name="scales2%d" % b, align_bytes=64)
            nc.vector.quantize_mx(out=codes[:].bitcast(FP8X4), scales=scales[:], in_=grouped2[:, b * P : (b + 1) * P, :].rearrange("p n t -> p (n t)"))
            quantised2.append((codes, scales))

        clutter = []
        for b in range(2):
            g = share.tile([P, S], F32, name="g%d" % b, offset=2048 + 2048 * b)
            nc.vector.tensor_copy(g[:], cm[b][:].indirect(cell_t[:]))
            clutter.append(g)

        sq2, z, df = {}, {}, {}

        def square(b, h):
            prod = psum.tile([P, 2, P], F32, name="prod2", tag="bank%d%d" % (b, h))
            for r in range(2):
                product(prod[:, r, :], 2 * h + r, *quantised2[b])
            sq2[b, h] = keep.tile([P, 2, P], F32, name="sq2", tag="piece%d%d" % (b, h))
            nc.scalar.activation(out=sq2[b, h][:], in_=prod[:], func=ACT.Square)

        def log_power(b, h):
            power = psum.tile([P, 2, P], F32, name="power", tag="bank%d%d" % (b, h))
            for r in range(2):
                nc.tensor.matmul(power[:, r, :], lhsT=sq1[h][:, r, b * P : (b + 1) * P], rhs=ident[:], is_transpose=True, start=r == 0, stop=False)
            for r in range(2):
                nc.tensor.matmul(power[:, r, :], lhsT=sq2[b, h][:, r, :], rhs=ident[:], is_transpose=True, start=False, stop=r == 1)
            z[b, h] = keep.tile([P, HALF], F32, name="z%d%d" % (b, h))
            nc.scalar.activation(out=z[b, h][:], in_=power[:].rearrange("p r n -> p (r n)"), func=ACT.Ln, bias=0.1)

        def excess(b, h):
            df[b, h] = keep.tile([P, HALF], F32, name="df%d%d" % (b, h))
            nc.vector.scalar_tensor_tensor(
                out=df[b, h][:], in0=z[b, h][:], scalar=thr_t[:, b : b + 1], in1=clutter[b][:, h * HALF : (h + 1) * HALF],
                op0=ALU.add, op1=ALU.subtract,
            )

        def finish(b, h):
            if b == h:
                res = keep.tile([P, HALF], F32, name="res%d%d" % (b, h))
                nc.vector.tensor_scalar(out=res[:], in0=df[b, h][:], scalar1=0.0, scalar2=None, op0=ALU.max)
            else:
                res = keep.tile([P, HALF], F32, name="res", tag="piece%d1" % (1 - b))
                nc.scalar.activation(out=res[:], in_=df[b, h][:], func=ACT.Relu)
            nc.sync.dma_start(out=out[b * P : (b + 1) * P, h * HALF : (h + 1) * HALF], in_=res[:])

        for i in range(len(pieces) + 3):
            if i >= 3:
                log_power(*pieces[i - 3])
            if i < len(pieces):
                square(*pieces[i])
        for i in range(len(pieces) + 1):
            if i < len(pieces):
                excess(*pieces[i])
            if i >= 1:
                finish(*pieces[i - 1])
